import numpy as np
import ml_dtypes

BF16 = ml_dtypes.bfloat16


def bf(x):
    return np.asarray(x, np.float32).astype(BF16)


def f32(x):
    return np.asarray(x, np.float32)


def f64(x):
    return np.asarray(x).astype(np.float64)


def striped(idx):
    return np.tile(idx.reshape(-1, 16).T, (8, 1))


S, K, M, N, D, V = 1024, 256, 512, 384, 2, 192


def setup_inputs():
    return {"table": bf(np.random.standard_normal((K, S))), "w": bf(np.random.standard_normal((D, K, M)) / np.sqrt(D * K)), "b": f32(0.5 * np.random.standard_normal((M, 1))), "offs": striped(np.random.permutation(S)[:N])}


def reference(table, w, b, offs):
    idx = offs[:16].T.reshape(-1)
    x = f64(table)[:, idx]
    y = sum(f64(w)[t].T @ x[:, t * V : (t + 1) * V] for t in range(D))
    return np.maximum(y + f64(b), 0.0)

@@ -1,0 +1,57 @@
+import concourse.mybir as mybir
+
+BF16, F32, U16 = mybir.dt.bfloat16, mybir.dt.float32, mybir.dt.uint16
+ADD, MAX = mybir.AluOpType.add, mybir.AluOpType.max
+
+P = 128
+NODES = 1024
+FEATURES = 256
+ENDS = 2
+EDGES = 192
+OUT_ROWS = 512
+FEATURE_BLOCKS = FEATURES // P
+OUT_BLOCKS = OUT_ROWS // P
+END_COLUMNS = EDGES // 16
+
+FLOPS = 2 * ENDS * FEATURES * OUT_ROWS * EDGES
+
+
+def tile_gather_matmul_kernel(tc, table, w, b, offs, out):
+    nc = tc.nc
+    with (
+        tc.tile_pool(name="held", bufs=1) as held,
+        tc.tile_pool(name="results", bufs=OUT_BLOCKS) as results,
+        tc.psum_pool(name="psum", bufs=1) as psum,
+    ):
+        offsets = held.tile([P, ENDS * END_COLUMNS], U16, name="offsets")
+        nc.sync.dma_start(offsets[:], offs)
+
+        windows = [held.tile([P, NODES], BF16, name=f"window{k}") for k in range(FEATURE_BLOCKS)]
+        for k in range(FEATURE_BLOCKS):
+            nc.sync.dma_start(windows[k][:], table[k * P : (k + 1) * P, :])
+
+        weights = [
+            [held.tile([P, OUT_ROWS], BF16, name=f"weights{t}{k}") for k in range(FEATURE_BLOCKS)]
+            for t in range(ENDS)
+        ]
+        for t in range(ENDS):
+            for k in range(FEATURE_BLOCKS):
+                nc.scalar.dma_start(weights[t][k][:], w[t, k * P : (k + 1) * P, :])
+
+        bias = held.tile([P, OUT_BLOCKS], F32, name="bias")
+        nc.scalar.dma_start(bias[:], b.rearrange("(a p) o -> p (a o)", p=P))
+
+        for a in range(OUT_BLOCKS):
+            bank = psum.tile([P, EDGES], F32, name=f"bank{a}")
+            for t in range(ENDS):
+                for k in range(FEATURE_BLOCKS):
+                    nc.tensor.matmul(
+                        bank[:],
+                        weights[t][k][:, a * P : (a + 1) * P],
+                        windows[k][:].indirect(offsets[:, t * END_COLUMNS : (t + 1) * END_COLUMNS]),
+                        start=(t == 0 and k == 0),
+                        stop=(t == ENDS - 1 and k == FEATURE_BLOCKS - 1),
+                    )
+            result = results.tile([P, EDGES], F32, name="result")
+            nc.vector.tensor_scalar(result[:], bank[:], bias[:, a : a + 1], 0.0, ADD, MAX)
+            nc.sync.dma_start(out[a * P : (a + 1) * P, :], result[:])

@@ -12,6 +12,8 @@ OUT_ROWS = 512
 FEATURE_BLOCKS = FEATURES // P
 OUT_BLOCKS = OUT_ROWS // P
 END_COLUMNS = EDGES // 16
+BANK = 512
+WARM_UPS = 5
 
 FLOPS = 2 * ENDS * FEATURES * OUT_ROWS * EDGES
 
@@ -40,6 +42,12 @@ def tile_gather_matmul_kernel(tc, table, w, b, offs, out):
 
         bias = held.tile([P, OUT_BLOCKS], F32, name="bias")
         nc.scalar.dma_start(bias[:], b.rearrange("(a p) o -> p (a o)", p=P))
+
+        zeros = held.tile([P, BANK], BF16, name="zeros")
+        nc.vector.memset(zeros[:], 0.0)
+        unread = psum.tile([P, BANK], F32, name="unread")
+        for i in range(WARM_UPS):
+            nc.tensor.matmul(unread[:], zeros[:, 0:P], zeros[:], start=True, stop=True)
 
         for a in range(OUT_BLOCKS):
             bank = psum.tile([P, EDGES], F32, name=f"bank{a}")

@@ -12,8 +12,6 @@ OUT_ROWS = 512
 FEATURE_BLOCKS = FEATURES // P
 OUT_BLOCKS = OUT_ROWS // P
 END_COLUMNS = EDGES // 16
-BANK = 512
-WARM_UPS = 5
 
 FLOPS = 2 * ENDS * FEATURES * OUT_ROWS * EDGES
 
@@ -36,18 +34,11 @@ def tile_gather_matmul_kernel(tc, table, w, b, offs, out):
             [held.tile([P, OUT_ROWS], BF16, name=f"weights{t}{k}") for k in range(FEATURE_BLOCKS)]
             for t in range(ENDS)
         ]
+        bias = held.tile([P, OUT_BLOCKS], F32, name="bias")
         for t in range(ENDS):
             for k in range(FEATURE_BLOCKS):
                 nc.scalar.dma_start(weights[t][k][:], w[t, k * P : (k + 1) * P, :])
-
-        bias = held.tile([P, OUT_BLOCKS], F32, name="bias")
         nc.scalar.dma_start(bias[:], b.rearrange("(a p) o -> p (a o)", p=P))
-
-        zeros = held.tile([P, BANK], BF16, name="zeros")
-        nc.vector.memset(zeros[:], 0.0)
-        unread = psum.tile([P, BANK], F32, name="unread")
-        for i in range(WARM_UPS):
-            nc.tensor.matmul(unread[:], zeros[:, 0:P], zeros[:], start=True, stop=True)
 
         for a in range(OUT_BLOCKS):
             bank = psum.tile([P, EDGES], F32, name=f"bank{a}")

@@ -12,6 +12,8 @@ OUT_ROWS = 512
 FEATURE_BLOCKS = FEATURES // P
 OUT_BLOCKS = OUT_ROWS // P
 END_COLUMNS = EDGES // 16
+HALF_NODES = NODES // 2
+HALF_ROWS = OUT_ROWS // 2
 
 FLOPS = 2 * ENDS * FEATURES * OUT_ROWS * EDGES
 
@@ -24,33 +26,36 @@ def tile_gather_matmul_kernel(tc, table, w, b, offs, out):
         tc.psum_pool(name="psum", bufs=1) as psum,
     ):
         offsets = held.tile([P, ENDS * END_COLUMNS], U16, name="offsets")
-        nc.sync.dma_start(offsets[:], offs)
-
         windows = [held.tile([P, NODES], BF16, name=f"window{k}") for k in range(FEATURE_BLOCKS)]
-        for k in range(FEATURE_BLOCKS):
-            nc.sync.dma_start(windows[k][:], table[k * P : (k + 1) * P, :])
-
         weights = [
             [held.tile([P, OUT_ROWS], BF16, name=f"weights{t}{k}") for k in range(FEATURE_BLOCKS)]
             for t in range(ENDS)
         ]
         bias = held.tile([P, OUT_BLOCKS], F32, name="bias")
-        for t in range(ENDS):
-            for k in range(FEATURE_BLOCKS):
-                nc.scalar.dma_start(weights[t][k][:], w[t, k * P : (k + 1) * P, :])
+
+        nc.sync.dma_start(windows[0][:, 0:HALF_NODES], table[0:P, 0:HALF_NODES])
+        nc.scalar.dma_start(windows[0][:, HALF_NODES:NODES], table[0:P, HALF_NODES:NODES])
+        nc.sync.dma_start(offsets[:], offs)
+        nc.sync.dma_start(weights[0][0][:, 0:HALF_ROWS], w[0, 0:P, 0:HALF_ROWS])
+        nc.scalar.dma_start(weights[0][0][:, HALF_ROWS:OUT_ROWS], w[0, 0:P, HALF_ROWS:OUT_ROWS])
+        nc.scalar.dma_start(weights[1][0][:], w[1, 0:P, :])
+        nc.sync.dma_start(windows[1][:], table[P : 2 * P, :])
+        nc.scalar.dma_start(weights[0][1][:], w[0, P : 2 * P, :])
+        nc.sync.dma_start(weights[1][1][:], w[1, P : 2 * P, :])
         nc.scalar.dma_start(bias[:], b.rearrange("(a p) o -> p (a o)", p=P))
 
-        for a in range(OUT_BLOCKS):
-            bank = psum.tile([P, EDGES], F32, name=f"bank{a}")
+        banks = [psum.tile([P, EDGES], F32, name=f"bank{a}") for a in range(OUT_BLOCKS)]
+        for k in range(FEATURE_BLOCKS):
             for t in range(ENDS):
-                for k in range(FEATURE_BLOCKS):
+                for a in range(OUT_BLOCKS):
                     nc.tensor.matmul(
-                        bank[:],
+                        banks[a][:],
                         weights[t][k][:, a * P : (a + 1) * P],
                         windows[k][:].indirect(offsets[:, t * END_COLUMNS : (t + 1) * END_COLUMNS]),
-                        start=(t == 0 and k == 0),
-                        stop=(t == ENDS - 1 and k == FEATURE_BLOCKS - 1),
+                        start=(k == 0 and t == 0),
+                        stop=(k == FEATURE_BLOCKS - 1 and t == ENDS - 1),
                     )
+        for a in range(OUT_BLOCKS):
             result = results.tile([P, EDGES], F32, name="result")
-            nc.vector.tensor_scalar(result[:], bank[:], bias[:, a : a + 1], 0.0, ADD, MAX)
+            nc.vector.tensor_scalar(result[:], banks[a][:], bias[:, a : a + 1], 0.0, ADD, MAX)
             nc.sync.dma_start(out[a * P : (a + 1) * P, :], result[:])

@@ -14,6 +14,7 @@ OUT_BLOCKS = OUT_ROWS // P
 END_COLUMNS = EDGES // 16
 HALF_NODES = NODES // 2
 HALF_ROWS = OUT_ROWS // 2
+PAIRS = OUT_ROWS // HALF_ROWS
 
 FLOPS = 2 * ENDS * FEATURES * OUT_ROWS * EDGES
 
@@ -27,35 +28,47 @@ def tile_gather_matmul_kernel(tc, table, w, b, offs, out):
     ):
         offsets = held.tile([P, ENDS * END_COLUMNS], U16, name="offsets")
         windows = [held.tile([P, NODES], BF16, name=f"window{k}") for k in range(FEATURE_BLOCKS)]
-        weights = [
-            [held.tile([P, OUT_ROWS], BF16, name=f"weights{t}{k}") for k in range(FEATURE_BLOCKS)]
-            for t in range(ENDS)
-        ]
+        first_weights = [held.tile([P, OUT_ROWS], BF16, name=f"first_weights{t}") for t in range(ENDS)]
+        last_weights = [held.tile([P, ENDS, HALF_ROWS], BF16, name=f"last_weights{h}") for h in range(PAIRS)]
         bias = held.tile([P, OUT_BLOCKS], F32, name="bias")
 
         nc.sync.dma_start(windows[0][:, 0:HALF_NODES], table[0:P, 0:HALF_NODES])
         nc.scalar.dma_start(windows[0][:, HALF_NODES:NODES], table[0:P, HALF_NODES:NODES])
         nc.sync.dma_start(offsets[:], offs)
-        nc.sync.dma_start(weights[0][0][:, 0:HALF_ROWS], w[0, 0:P, 0:HALF_ROWS])
-        nc.scalar.dma_start(weights[0][0][:, HALF_ROWS:OUT_ROWS], w[0, 0:P, HALF_ROWS:OUT_ROWS])
-        nc.scalar.dma_start(weights[1][0][:], w[1, 0:P, :])
+        nc.sync.dma_start(first_weights[0][:, 0:HALF_ROWS], w[0, 0:P, 0:HALF_ROWS])
+        nc.scalar.dma_start(first_weights[0][:, HALF_ROWS:OUT_ROWS], w[0, 0:P, HALF_ROWS:OUT_ROWS])
+        nc.scalar.dma_start(first_weights[1][:], w[1, 0:P, :])
         nc.sync.dma_start(windows[1][:], table[P : 2 * P, :])
-        nc.scalar.dma_start(weights[0][1][:], w[0, P : 2 * P, :])
-        nc.sync.dma_start(weights[1][1][:], w[1, P : 2 * P, :])
+        pair_queues = [nc.scalar, nc.sync]
+        for h in range(PAIRS):
+            pair_queues[h].dma_start(
+                last_weights[h][:],
+                w[:, P : 2 * P, h * HALF_ROWS : (h + 1) * HALF_ROWS].rearrange("t p m -> p t m"),
+            )
         nc.scalar.dma_start(bias[:], b.rearrange("(a p) o -> p (a o)", p=P))
 
         banks = [psum.tile([P, EDGES], F32, name=f"bank{a}") for a in range(OUT_BLOCKS)]
-        for k in range(FEATURE_BLOCKS):
+        picked = [
+            [windows[k][:].indirect(offsets[:, t * END_COLUMNS : (t + 1) * END_COLUMNS]) for k in range(FEATURE_BLOCKS)]
+            for t in range(ENDS)
+        ]
+        for t in range(ENDS):
+            for a in range(OUT_BLOCKS):
+                nc.tensor.matmul(
+                    banks[a][:], first_weights[t][:, a * P : (a + 1) * P], picked[t][0], start=(t == 0), stop=False
+                )
+        for h in range(PAIRS):
             for t in range(ENDS):
-                for a in range(OUT_BLOCKS):
+                for c in range(OUT_BLOCKS // PAIRS):
                     nc.tensor.matmul(
-                        banks[a][:],
-                        weights[t][k][:, a * P : (a + 1) * P],
-                        windows[k][:].indirect(offsets[:, t * END_COLUMNS : (t + 1) * END_COLUMNS]),
-                        start=(k == 0 and t == 0),
-                        stop=(k == FEATURE_BLOCKS - 1 and t == ENDS - 1),
+                        banks[h * (OUT_BLOCKS // PAIRS) + c][:],
+                        last_weights[h][:, t, c * P : (c + 1) * P],
+                        picked[t][1],
+                        start=False,
+                        stop=(t == ENDS - 1),
                     )
-        for a in range(OUT_BLOCKS):
-            result = results.tile([P, EDGES], F32, name="result")
-            nc.vector.tensor_scalar(result[:], banks[a][:], bias[:, a : a + 1], 0.0, ADD, MAX)
-            nc.sync.dma_start(out[a * P : (a + 1) * P, :], result[:])
+            for c in range(OUT_BLOCKS // PAIRS):
+                a = h * (OUT_BLOCKS // PAIRS) + c
+                result = results.tile([P, EDGES], F32, name="result")
+                nc.vector.tensor_scalar(result[:], banks[a][:], bias[:, a : a + 1], 0.0, ADD, MAX)
+                nc.sync.dma_start(out[a * P : (a + 1) * P, :], result[:])

@@ -39,11 +39,11 @@ def tile_gather_matmul_kernel(tc, table, w, b, offs, out):
         nc.scalar.dma_start(first_weights[0][:, HALF_ROWS:OUT_ROWS], w[0, 0:P, HALF_ROWS:OUT_ROWS])
         nc.scalar.dma_start(first_weights[1][:], w[1, 0:P, :])
         nc.sync.dma_start(windows[1][:], table[P : 2 * P, :])
-        pair_queues = [nc.scalar, nc.sync]
-        for h in range(PAIRS):
-            pair_queues[h].dma_start(
-                last_weights[h][:],
-                w[:, P : 2 * P, h * HALF_ROWS : (h + 1) * HALF_ROWS].rearrange("t p m -> p t m"),
+        nc.scalar.dma_start(last_weights[0][:], w[:, P : 2 * P, 0:HALF_ROWS].rearrange("t p m -> p t m"))
+        for c in range(OUT_BLOCKS // PAIRS):
+            nc.sync.dma_start(
+                last_weights[1][:, :, c * P : (c + 1) * P],
+                w[:, P : 2 * P, HALF_ROWS + c * P : HALF_ROWS + (c + 1) * P].rearrange("t p m -> p t m"),
             )
         nc.scalar.dma_start(bias[:], b.rearrange("(a p) o -> p (a o)", p=P))
 

import concourse.mybir as mybir

BF16, F32, U16 = mybir.dt.bfloat16, mybir.dt.float32, mybir.dt.uint16
ADD, MAX = mybir.AluOpType.add, mybir.AluOpType.max

P = 128
NODES = 1024
FEATURES = 256
ENDS = 2
EDGES = 192
OUT_ROWS = 512
FEATURE_BLOCKS = FEATURES // P
OUT_BLOCKS = OUT_ROWS // P
END_COLUMNS = EDGES // 16
HALF_NODES = NODES // 2
HALF_ROWS = OUT_ROWS // 2
PAIRS = OUT_ROWS // HALF_ROWS

FLOPS = 2 * ENDS * FEATURES * OUT_ROWS * EDGES


def tile_gather_matmul_kernel(tc, table, w, b, offs, out):
    nc = tc.nc
    with (
        tc.tile_pool(name="held", bufs=1) as held,
        tc.tile_pool(name="results", bufs=OUT_BLOCKS) as results,
        tc.psum_pool(name="psum", bufs=1) as psum,
    ):
        offsets = held.tile([P, ENDS * END_COLUMNS], U16, name="offsets")
        windows = [held.tile([P, NODES], BF16, name=f"window{k}") for k in range(FEATURE_BLOCKS)]
        first_weights = [held.tile([P, OUT_ROWS], BF16, name=f"first_weights{t}") for t in range(ENDS)]
        last_weights = [held.tile([P, ENDS, HALF_ROWS], BF16, name=f"last_weights{h}") for h in range(PAIRS)]
        bias = held.tile([P, OUT_BLOCKS], F32, name="bias")

        nc.sync.dma_start(windows[0][:, 0:HALF_NODES], table[0:P, 0:HALF_NODES])
        nc.scalar.dma_start(windows[0][:, HALF_NODES:NODES], table[0:P, HALF_NODES:NODES])
        nc.sync.dma_start(offsets[:], offs)
        nc.sync.dma_start(first_weights[0][:, 0:HALF_ROWS], w[0, 0:P, 0:HALF_ROWS])
        nc.scalar.dma_start(first_weights[0][:, HALF_ROWS:OUT_ROWS], w[0, 0:P, HALF_ROWS:OUT_ROWS])
        nc.scalar.dma_start(first_weights[1][:], w[1, 0:P, :])
        nc.sync.dma_start(windows[1][:], table[P : 2 * P, :])
        nc.scalar.dma_start(last_weights[0][:], w[:, P : 2 * P, 0:HALF_ROWS].rearrange("t p m -> p t m"))
        for c in range(OUT_BLOCKS // PAIRS):
            nc.sync.dma_start(
                last_weights[1][:, :, c * P : (c + 1) * P],
                w[:, P : 2 * P, HALF_ROWS + c * P : HALF_ROWS + (c + 1) * P].rearrange("t p m -> p t m"),
            )
        nc.scalar.dma_start(bias[:], b.rearrange("(a p) o -> p (a o)", p=P))

        banks = [psum.tile([P, EDGES], F32, name=f"bank{a}") for a in range(OUT_BLOCKS)]
        picked = [
            [windows[k][:].indirect(offsets[:, t * END_COLUMNS : (t + 1) * END_COLUMNS]) for k in range(FEATURE_BLOCKS)]
            for t in range(ENDS)
        ]
        for t in range(ENDS):
            for a in range(OUT_BLOCKS):
                nc.tensor.matmul(
                    banks[a][:], first_weights[t][:, a * P : (a + 1) * P], picked[t][0], start=(t == 0), stop=False
                )
        for h in range(PAIRS):
            for t in range(ENDS):
                for c in range(OUT_BLOCKS // PAIRS):
                    nc.tensor.matmul(
                        banks[h * (OUT_BLOCKS // PAIRS) + c][:],
                        last_weights[h][:, t, c * P : (c + 1) * P],
                        picked[t][1],
                        start=False,
                        stop=(t == ENDS - 1),
                    )
            for c in range(OUT_BLOCKS // PAIRS):
                a = h * (OUT_BLOCKS // PAIRS) + c
                result = results.tile([P, EDGES], F32, name="result")
                nc.vector.tensor_scalar(result[:], banks[a][:], bias[:, a : a + 1], 0.0, ADD, MAX)
                nc.sync.dma_start(out[a * P : (a + 1) * P, :], result[:])
